import numpy as np
import ml_dtypes


def mxq(x, axis, fmt="e4m3"):
    dtype, down = {"e4m3": (ml_dtypes.float8_e4m3fn, 7), "e5m2": (ml_dtypes.float8_e5m2, 14)}[fmt]
    v = np.moveaxis(np.asarray(x, np.float32).astype(ml_dtypes.bfloat16).astype(np.float64), axis, -1)
    blocks = v.reshape(v.shape[:-1] + (-1, 32))
    amax = np.abs(blocks).max(-1, keepdims=True)
    byte = np.maximum(np.where(amax > 0, np.frexp(amax)[1] - 1 + 127, 0) - down, 1)
    scale = np.exp2(byte - 127.0)
    codes = (blocks / scale).astype(np.float32).astype(dtype).astype(np.float64)
    return np.moveaxis((codes * scale).reshape(v.shape), -1, axis)


WIDE = False


def mx_kscale(k):
    if not WIDE:
        return np.ones(k)
    levels = np.array([30, -30])
    if k % 512:
        return np.exp2(np.random.permutation(np.resize(levels, k // 32))).repeat(32)
    a = np.empty((k // 512, 16))
    for p in range(k // 512):
        a[p, :8] = np.random.permutation(np.resize(levels, 8))
        for g in range(8):
            far = levels[np.abs(levels - a[p, g]) >= 10]
            a[p, g + 8] = far[np.random.randint(len(far))]
    return np.exp2(a.ravel()).repeat(32)


def f64(x):
    return np.asarray(x).astype(np.float64)


def striped(idx):
    return np.tile(np.asarray(idx).reshape(-1, 16).T, (8, 1)).astype(np.uint16)


def unstriped(offs):
    return offs[:16].T.reshape(-1).astype(np.int64)


E2M1 = np.array([0.0, 0.5, 1.0, 1.5, 2.0, 3.0, 4.0, 6.0, -0.0, -0.5, -1.0, -1.5, -2.0, -3.0, -4.0, -6.0])


def pack_weight(w, fmt):
    k, n = w.shape
    w = f64(np.asarray(w, np.float32).astype(ml_dtypes.bfloat16)).reshape(k // 32, 32, n)
    amax = np.abs(w).max(1)
    if fmt in ("e4m3", "e5m2"):
        byte = np.frexp(amax)[1] - 1 + 127 - (7 if fmt == "e4m3" else 14)
    else:
        mant, ex = np.frexp(amax / 6.0)
        byte = np.where(mant > 0.5, ex, ex - 1) + 127
    byte = np.clip(np.where(amax > 0, byte, 1), 1, 254)
    scaled = (w * np.exp2(127.0 - byte)[:, None, :]).reshape(k, n).astype(np.float32)
    by_word = np.ascontiguousarray(scaled.reshape(k // 512, 128, 4, n).transpose(0, 1, 3, 2))
    if fmt in ("e4m3", "e5m2"):
        words = by_word.astype(ml_dtypes.float8_e4m3fn if fmt == "e4m3" else ml_dtypes.float8_e5m2).view(np.uint8)
    else:
        c = by_word.astype(ml_dtypes.float4_e2m1fn).view(np.uint8) & 0xF
        words = (c[..., 0::2] | (c[..., 1::2] << 4)).reshape(k // 512, 128, 2 * n)
    return np.ascontiguousarray(words), np.ascontiguousarray(byte.astype(np.uint8).reshape(k // 512, 16, n))


def unpack_weight(words, scales, fmt):
    g, _, n = scales.shape
    words = np.ascontiguousarray(words).reshape(g, 128, n, -1)
    if fmt in ("e4m3", "e5m2"):
        vals = words.view(ml_dtypes.float8_e4m3fn if fmt == "e4m3" else ml_dtypes.float8_e5m2).astype(np.float64)
    else:
        nib = np.empty((g, 128, n, 4), np.uint8)
        nib[..., 0::2] = words & 0xF
        nib[..., 1::2] = words >> 4
        vals = E2M1[nib]
    vals = vals * np.repeat(np.exp2(scales.astype(np.float64) - 127.0), 8, axis=1)[..., None]
    return vals.transpose(0, 1, 3, 2).reshape(g * 512, n)


def bf(x):
    return np.asarray(x, np.float32).astype(ml_dtypes.bfloat16)


def planes(Y):
    r, m = Y.shape
    b = f64(bf(Y)).reshape(r // 32, 32, m)
    amax = np.abs(b).max(1)
    byte = np.clip(np.where(amax > 0, np.frexp(amax)[1] - 1 + 127 - 7, 1), 1, 254)
    codes = (b * np.exp2(127.0 - byte)[:, None, :]).reshape(r, m).astype(np.float32).astype(ml_dtypes.float8_e4m3fn).view(np.uint8)
    words = codes.reshape(r // 512, 128, 4, m).transpose(0, 1, 3, 2)
    return np.ascontiguousarray(words), np.ascontiguousarray(byte.astype(np.uint8).reshape(r // 512, 16, m))


K, T, J, R, N = 1024, 1024, 256, 512, 512


def setup_inputs():
    n = np.random.standard_normal
    idx = np.random.permutation(T)[:J]
    fk = mx_kscale(K)
    fr = mx_kscale(R)
    wp = pack_weight(n((K, R)) * 1 / np.sqrt(K) * fk[:, None] * fr, "e5m2")
    wbp = pack_weight(n((R, N)) * 1 / np.sqrt(R) / fr[:, None], "e2m1")
    return {
        "xf": (n((K, T))).astype(np.float32),
        "fk": (np.random.uniform(0.5, 2.0, (K, 1)) / fk[:, None]).astype(np.float32),
        "w_words": wp[0],
        "w_scales": wp[1],
        "us": (np.random.uniform(0.5, 2.0, (R, 1)) * fr[:, None]).astype(np.float32),
        "wb_words": wbp[0],
        "wb_scales": wbp[1],
        "hi": (np.random.uniform(0.4, 1.2, (N, 1))).astype(np.float32),
        "rw": (np.random.uniform(0.5, 2.0, (1, J))).astype(np.float32),
        "offs": striped(idx),
    }


def reference(xf, fk, w_words, w_scales, us, wb_words, wb_scales, hi, rw, offs):
    idx = unstriped(offs)
    wu = unpack_weight(w_words, w_scales, "e5m2")
    wbu = unpack_weight(wb_words, wb_scales, "e2m1")
    xg = f64(xf)[:, idx]
    x1 = np.pad(xg, ((0, 0), (1, 0)))[:, :J]
    u = (xg - 0.6 * x1) * f64(fk)
    uq = mxq(u, 0, "e5m2")
    a = wu.T @ uq
    pk1 = np.max(np.abs(a), axis=1, keepdims=True)
    hid = a / pk1 * f64(us)
    hidq = mxq(hid, 0, "e5m2")
    p = wbu.T @ hidq
    y = np.minimum(p - f64(hi), 0.0) * f64(rw)
    words, scales = planes(y)
    return y, words, scales

@@ -1,0 +1,240 @@
+from contextlib import ExitStack
+
+import concourse.mybir as mybir
+
+K, T, J, R, N = 1024, 1024, 256, 512, 512
+FLOPS = 2 * K * R * J + 2 * R * N * J
+
+F32 = mybir.dt.float32
+BF16 = mybir.dt.bfloat16
+I32 = mybir.dt.int32
+U32 = mybir.dt.uint32
+U16 = mybir.dt.uint16
+U8 = mybir.dt.uint8
+E5M2X4 = mybir.dt.float8_e5m2_x4
+E4M3X4 = mybir.dt.float8_e4m3fn_x4
+E2M1X4 = mybir.dt.float4_e2m1fn_x4
+ALU = mybir.AluOpType
+ACT = mybir.ActivationFunctionType
+AXIS = mybir.AxisListType
+
+P = 128
+PACK = 4
+PASSES = K // (P * PACK)
+QUADS = 4
+LEAD = 8
+HALF = J // 2
+WALK = 4
+
+
+def tile_list_steps_peakscaled_capped_pl_kernel(
+    tc, xf, fk, w_words, w_scales, us, wb_words, wb_scales, hi, rw, offs, out_0, out_1, out_2
+):
+    nc = tc.nc
+    with ExitStack() as ctx:
+        sb = ctx.enter_context(tc.tile_pool(name="sb", bufs=1))
+        ps = ctx.enter_context(tc.psum_pool(name="ps", bufs=1))
+
+        offsets = sb.tile([P, J // 16], U16, name="offsets")
+        w_raw = sb.tile([P, PASSES, R], I32, name="w_raw")
+        ws_raw = sb.tile([P, PASSES, R // 4], I32, name="ws_raw")
+        wb_raw = sb.tile([P, N // 2], I32, name="wb_raw")
+        wbs_raw = sb.tile([P, N // 4], I32, name="wbs_raw")
+        fk_sb = sb.tile([P, PASSES, PACK], F32, name="fk_sb")
+        us_sb = sb.tile([P, PACK], F32, name="us_sb")
+        hi_sb = sb.tile([P, PACK], F32, name="hi_sb")
+        rw_sb = sb.tile([P, J], F32, name="rw_sb")
+        picked = sb.tile([P, PASSES * PACK, LEAD + J], F32, name="picked")
+
+        nc.vector.memset(ws_raw[:], 0)
+        nc.vector.memset(wbs_raw[:], 0)
+        nc.vector.memset(picked[:, :, LEAD - 1 : LEAD], 0.0)
+
+        x_rows = xf.rearrange("(g p t) c -> g p t c", g=PASSES, t=PACK)
+        groups = [(0, 0, 2), (0, 2, 2), (1, 0, 2), (1, 2, 1), (1, 3, 1)]
+        x_tiles = [sb.tile([P, n, T], F32, name="x_%d_%d" % (g, t0)) for g, t0, n in groups]
+
+        def load_x(i):
+            g, t0, n = groups[i]
+            nc.sync.dma_start(out=x_tiles[i][:], in_=x_rows[g, :, t0 : t0 + n, :])
+
+        nc.sync.dma_start(out=w_raw[:], in_=w_words.rearrange("g p n t -> p g (n t)").bitcast(I32))
+        ws_dram = w_scales.rearrange("g q c -> q g c").bitcast(I32)
+        for q in range(QUADS):
+            nc.sync.dma_start(out=ws_raw[32 * q : 32 * q + 4, :, :], in_=ws_dram[4 * q : 4 * q + 4, :, :])
+        nc.sync.dma_start(offsets[:], offs)
+        load_x(0)
+        load_x(1)
+        nc.sync.dma_start(out=fk_sb[:], in_=fk.rearrange("(g p t) o -> p g (t o)", g=PASSES, t=PACK))
+        nc.sync.dma_start(out=wb_raw[:], in_=wb_words[0].bitcast(I32))
+        wbs_dram = wb_scales[0].bitcast(I32)
+        for q in range(QUADS):
+            nc.sync.dma_start(out=wbs_raw[32 * q : 32 * q + 4, :], in_=wbs_dram[4 * q : 4 * q + 4, :])
+        load_x(2)
+        load_x(3)
+        load_x(4)
+        nc.sync.dma_start(out=us_sb[:], in_=us.rearrange("(p t) o -> p (t o)", t=PACK))
+        nc.sync.dma_start(out=hi_sb[:], in_=hi.rearrange("(p t) o -> p (t o)", t=PACK))
+        nc.sync.dma_start(out=rw_sb[:], in_=rw[0].partition_broadcast(P))
+
+        w_codes = sb.tile([P, PASSES, R], U32, name="w_codes", align_bytes=64)
+        w_plane = sb.tile([P, PASSES, R], U8, name="w_plane", align_bytes=64)
+        wb_codes = sb.tile([P, N], U16, name="wb_codes", align_bytes=64)
+        wb_plane = sb.tile([P, N], U8, name="wb_plane", align_bytes=64)
+        nc.vector.tensor_copy(
+            out=w_codes[:].rearrange("p g (t m) -> p g m t", t=PACK),
+            in_=w_raw[:].bitcast(U32).rearrange("p g (m t) -> p g m t", t=PACK),
+        )
+        nc.vector.tensor_copy(
+            out=w_plane[:].rearrange("p g (t m) -> p g m t", t=PACK),
+            in_=ws_raw[:].bitcast(U8).rearrange("p g (m t) -> p g m t", t=PACK),
+        )
+        nc.vector.tensor_copy(
+            out=wb_codes[:].rearrange("p (t m) -> p m t", t=PACK),
+            in_=wb_raw[:].bitcast(U16).rearrange("p (m t) -> p m t", t=PACK),
+        )
+        nc.vector.tensor_copy(
+            out=wb_plane[:].rearrange("p (t m) -> p m t", t=PACK),
+            in_=wbs_raw[:].bitcast(U8).rearrange("p (m t) -> p m t", t=PACK),
+        )
+
+        steps = sb.tile([P, PASSES * PACK, J], F32, name="steps")
+        u_bf = [sb.tile([P, J, PACK], BF16, name="u_bf%d" % g, align_bytes=64) for g in range(PASSES)]
+        u_codes = [sb.tile([P, J], U32, name="u_codes%d" % g, align_bytes=64) for g in range(PASSES)]
+        u_plane = [sb.tile([P, J], U8, name="u_plane%d" % g, align_bytes=64) for g in range(PASSES)]
+        a_ps = [ps.tile([P, J], F32, name="a_ps%d" % t) for t in range(PACK)]
+
+        def step_and_scale(g, t, spans):
+            s = g * PACK + t
+            for j0, j1 in spans:
+                nc.vector.scalar_tensor_tensor(
+                    out=steps[:, s, j0:j1],
+                    in0=picked[:, s, LEAD - 1 + j0 : LEAD - 1 + j1],
+                    scalar=-0.6,
+                    in1=picked[:, s, LEAD + j0 : LEAD + j1],
+                    op0=ALU.mult,
+                    op1=ALU.add,
+                )
+            for j0, j1 in spans:
+                nc.vector.tensor_scalar(
+                    out=u_bf[g][:, j0:j1, t],
+                    in0=steps[:, s, j0:j1],
+                    scalar1=fk_sb[:, g, t : t + 1],
+                    scalar2=None,
+                    op0=ALU.mult,
+                )
+
+        def quantise(codes, plane, grouped, fmt, spans):
+            for j0, j1 in spans:
+                nc.vector.quantize_mx(
+                    out=codes[:, j0:j1].bitcast(fmt),
+                    scales=plane[:, j0:j1],
+                    in_=grouped[:, j0:j1, :].rearrange("p j t -> p (j t)"),
+                )
+
+        whole = [(0, J)]
+        halves = [(0, HALF), (HALF, J)]
+        for i, (g, t0, n) in enumerate(groups):
+            for d in range(n):
+                t = t0 + d
+                s = g * PACK + t
+                window = x_tiles[i][:, d, :]
+                if i < len(groups) - 1:
+                    nc.scalar.activation(picked[:, s, LEAD:], window.indirect(offsets[:]), ACT.Copy)
+                    step_and_scale(g, t, whole)
+                else:
+                    cols = HALF // 16
+                    nc.vector.tensor_copy(picked[:, s, LEAD : LEAD + HALF], window.indirect(offsets[:, :cols]))
+                    nc.scalar.activation(picked[:, s, LEAD + HALF :], window.indirect(offsets[:, cols:]), ACT.Copy)
+                    step_and_scale(g, t, halves)
+            if t0 + n == PACK:
+                quantise(u_codes[g], u_plane[g], u_bf[g], E5M2X4, halves if g == PASSES - 1 else whole)
+                for t in range(PACK):
+                    cols = slice(t * P, (t + 1) * P)
+                    nc.tensor.matmul_mx(
+                        out=a_ps[t][:],
+                        lhsT=w_codes[:, g, cols].bitcast(E5M2X4),
+                        lhsT_scale=w_plane[:, g, cols],
+                        rhs=u_codes[g][:].bitcast(E5M2X4),
+                        rhs_scale=u_plane[g][:],
+                        start=(g == 0),
+                        stop=(g == PASSES - 1),
+                    )
+
+        a_sb = sb.tile([P, PACK, J], F32, name="a_sb")
+        peak = sb.tile([P, PACK], F32, name="peak")
+        inv_peak = sb.tile([P, PACK], F32, name="inv_peak")
+        gain = sb.tile([P, 2], F32, name="gain")
+        hid_rows = sb.tile([P, PACK, J], BF16, name="hid_rows")
+        hid_bf = sb.tile([P, J, PACK], BF16, name="hid_bf", align_bytes=64)
+        for t in range(PACK):
+            nc.scalar.activation(a_sb[:, t, :], a_ps[t][:], ACT.Copy)
+            nc.vector.tensor_reduce(
+                out=peak[:, t : t + 1], in_=a_sb[:, t, :], axis=AXIS.X, op=ALU.max, apply_absolute_value=True
+            )
+            if t == 1:
+                nc.vector.reciprocal(out=inv_peak[:, 0:2], in_=peak[:, 0:2])
+                nc.vector.tensor_tensor(out=gain[:], in0=inv_peak[:, 0:2], in1=us_sb[:, 0:2], op=ALU.mult)
+            elif t > 1:
+                nc.vector.reciprocal(out=inv_peak[:, t : t + 1], in_=peak[:, t : t + 1])
+        for t in range(PACK):
+            if t < 2:
+                nc.scalar.activation(hid_rows[:, t, :], a_sb[:, t, :], ACT.Copy, scale=gain[:, t : t + 1])
+            else:
+                nc.vector.tensor_scalar(
+                    out=hid_rows[:, t, :],
+                    in0=a_sb[:, t, :],
+                    scalar1=inv_peak[:, t : t + 1],
+                    scalar2=us_sb[:, t : t + 1],
+                    op0=ALU.mult,
+                    op1=ALU.mult,
+                )
+
+        def weave(copy, grouped, rows, j0, j1):
+            copy(
+                out=grouped[:, j0:j1, :].rearrange("p (c i) t -> p c t i", i=WALK),
+                in_=rows[:, :, j0:j1].rearrange("p t (c i) -> p c t i", i=WALK),
+            )
+
+        hid_codes = sb.tile([P, J], U32, name="hid_codes", align_bytes=64)
+        hid_plane = sb.tile([P, J], U8, name="hid_plane", align_bytes=64)
+        for j0, j1 in halves:
+            weave(nc.vector.tensor_copy, hid_bf, hid_rows, j0, j1)
+        quantise(hid_codes, hid_plane, hid_bf, E5M2X4, halves)
+
+        neg_hi = sb.tile([P, PACK], F32, name="neg_hi")
+        nc.scalar.activation(neg_hi[:], hi_sb[:], ACT.Copy, scale=-1.0)
+        p_ps = [ps.tile([P, J], F32, name="p_ps%d" % t) for t in range(PACK)]
+        excess = sb.tile([P, PACK, J], F32, name="excess")
+        y = sb.tile([P, PACK, J], F32, name="y")
+        out_rows = out_0.rearrange("(p t) j -> p t j", t=PACK)
+        for t in range(PACK):
+            nc.tensor.matmul_mx(
+                out=p_ps[t][:],
+                lhsT=wb_codes[:, t * P : (t + 1) * P].bitcast(E2M1X4),
+                lhsT_scale=wb_plane[:, t * P : (t + 1) * P],
+                rhs=hid_codes[:].bitcast(E5M2X4),
+                rhs_scale=hid_plane[:],
+                start=True,
+                stop=True,
+            )
+            nc.scalar.activation(excess[:, t, :], p_ps[t][:], ACT.Identity, bias=neg_hi[:, t : t + 1])
+            nc.vector.scalar_tensor_tensor(
+                out=y[:, t, :], in0=excess[:, t, :], scalar=0.0, in1=rw_sb[:], op0=ALU.min, op1=ALU.mult
+            )
+            if t % 2 == 1:
+                nc.sync.dma_start(out=out_rows[:, t - 1 : t + 1, :], in_=y[:, t - 1 : t + 1, :])
+
+        y_bf = sb.tile([P, J, PACK], BF16, name="y_bf", align_bytes=64)
+        y_codes = sb.tile([P, J], U32, name="y_codes", align_bytes=64)
+        y_plane = sb.tile([P, J], U8, name="y_plane", align_bytes=64)
+        split = 176
+        weave(nc.vector.tensor_copy, y_bf, y, 0, split)
+        weave(nc.scalar.copy, y_bf, y, split, J)
+        quantise(y_codes, y_plane, y_bf, E4M3X4, halves)
+        nc.sync.dma_start(out=out_1[0].rearrange("p c t -> p (c t)").bitcast(I32), in_=y_codes[:].bitcast(I32))
+        plane_words = y_plane[:].bitcast(I32)
+        scales_dram = out_2[0].bitcast(I32)
+        for q in range(QUADS):
+            queue = nc.scalar if q % 2 == 0 else nc.sync
+            queue.dma_start(out=scales_dram[4 * q : 4 * q + 4, :], in_=plane_words[32 * q : 32 * q + 4, :])

@@ -33,6 +33,7 @@ def tile_list_steps_peakscaled_capped_pl_kernel(
     nc = tc.nc
     with ExitStack() as ctx:
         sb = ctx.enter_context(tc.tile_pool(name="sb", bufs=1))
+        shared = ctx.enter_context(tc.tile_pool(name="shared", bufs=1))
         ps = ctx.enter_context(tc.psum_pool(name="ps", bufs=1))
 
         offsets = sb.tile([P, J // 16], U16, name="offsets")
@@ -48,39 +49,36 @@ def tile_list_steps_peakscaled_capped_pl_kernel(
 
         nc.vector.memset(ws_raw[:], 0)
         nc.vector.memset(wbs_raw[:], 0)
-        nc.vector.memset(picked[:, :, LEAD - 1 : LEAD], 0.0)
+        zeros = sb.tile([P, PASSES * PACK, 1], F32, name="zeros")
+        nc.vector.memset(zeros[:], 0.0)
+        nc.scalar.activation(picked[:, :, LEAD - 1 : LEAD], zeros[:], ACT.Copy)
 
         x_rows = xf.rearrange("(g p t) c -> g p t c", g=PASSES, t=PACK)
-        groups = [(0, 0, 2), (0, 2, 2), (1, 0, 2), (1, 2, 1), (1, 3, 1)]
+        groups = [(g, t, 1) for g in range(PASSES) for t in range(PACK)]
         x_tiles = [sb.tile([P, n, T], F32, name="x_%d_%d" % (g, t0)) for g, t0, n in groups]
 
         def load_x(i):
             g, t0, n = groups[i]
             nc.sync.dma_start(out=x_tiles[i][:], in_=x_rows[g, :, t0 : t0 + n, :])
 
+        nc.sync.dma_start(offsets[:], offs)
+        nc.sync.dma_start(out=fk_sb[:], in_=fk.rearrange("(g p t) o -> p g (t o)", g=PASSES, t=PACK))
         nc.sync.dma_start(out=w_raw[:], in_=w_words.rearrange("g p n t -> p g (n t)").bitcast(I32))
         ws_dram = w_scales.rearrange("g q c -> q g c").bitcast(I32)
         for q in range(QUADS):
             nc.sync.dma_start(out=ws_raw[32 * q : 32 * q + 4, :, :], in_=ws_dram[4 * q : 4 * q + 4, :, :])
-        nc.sync.dma_start(offsets[:], offs)
-        load_x(0)
-        load_x(1)
-        nc.sync.dma_start(out=fk_sb[:], in_=fk.rearrange("(g p t) o -> p g (t o)", g=PASSES, t=PACK))
+        for i in range(len(groups)):
+            load_x(i)
         nc.sync.dma_start(out=wb_raw[:], in_=wb_words[0].bitcast(I32))
         wbs_dram = wb_scales[0].bitcast(I32)
         for q in range(QUADS):
             nc.sync.dma_start(out=wbs_raw[32 * q : 32 * q + 4, :], in_=wbs_dram[4 * q : 4 * q + 4, :])
-        load_x(2)
-        load_x(3)
-        load_x(4)
         nc.sync.dma_start(out=us_sb[:], in_=us.rearrange("(p t) o -> p (t o)", t=PACK))
         nc.sync.dma_start(out=hi_sb[:], in_=hi.rearrange("(p t) o -> p (t o)", t=PACK))
         nc.sync.dma_start(out=rw_sb[:], in_=rw[0].partition_broadcast(P))
 
         w_codes = sb.tile([P, PASSES, R], U32, name="w_codes", align_bytes=64)
         w_plane = sb.tile([P, PASSES, R], U8, name="w_plane", align_bytes=64)
-        wb_codes = sb.tile([P, N], U16, name="wb_codes", align_bytes=64)
-        wb_plane = sb.tile([P, N], U8, name="wb_plane", align_bytes=64)
         nc.vector.tensor_copy(
             out=w_codes[:].rearrange("p g (t m) -> p g m t", t=PACK),
             in_=w_raw[:].bitcast(U32).rearrange("p g (m t) -> p g m t", t=PACK),
@@ -89,17 +87,12 @@ def tile_list_steps_peakscaled_capped_pl_kernel(
             out=w_plane[:].rearrange("p g (t m) -> p g m t", t=PACK),
             in_=ws_raw[:].bitcast(U8).rearrange("p g (m t) -> p g m t", t=PACK),
         )
-        nc.vector.tensor_copy(
-            out=wb_codes[:].rearrange("p (t m) -> p m t", t=PACK),
-            in_=wb_raw[:].bitcast(U16).rearrange("p (m t) -> p m t", t=PACK),
-        )
-        nc.vector.tensor_copy(
-            out=wb_plane[:].rearrange("p (t m) -> p m t", t=PACK),
-            in_=wbs_raw[:].bitcast(U8).rearrange("p (m t) -> p m t", t=PACK),
-        )
 
         steps = sb.tile([P, PASSES * PACK, J], F32, name="steps")
-        u_bf = [sb.tile([P, J, PACK], BF16, name="u_bf%d" % g, align_bytes=64) for g in range(PASSES)]
+        u_bf = [
+            shared.tile([P, J, PACK], BF16, name="u_bf%d" % g, align_bytes=64, offset=g * J * PACK * 2)
+            for g in range(PASSES)
+        ]
         u_codes = [sb.tile([P, J], U32, name="u_codes%d" % g, align_bytes=64) for g in range(PASSES)]
         u_plane = [sb.tile([P, J], U8, name="u_plane%d" % g, align_bytes=64) for g in range(PASSES)]
         a_ps = [ps.tile([P, J], F32, name="a_ps%d" % t) for t in range(PACK)]
@@ -160,6 +153,18 @@ def tile_list_steps_peakscaled_capped_pl_kernel(
                         start=(g == 0),
                         stop=(g == PASSES - 1),
                     )
+
+        last = (PASSES - 1) * J * PACK * 2
+        wb_codes = shared.tile([P, N], U16, name="wb_codes", align_bytes=64, offset=last)
+        wb_plane = shared.tile([P, N], U8, name="wb_plane", align_bytes=64, offset=last + 2 * N)
+        nc.vector.tensor_copy(
+            out=wb_codes[:].rearrange("p (t m) -> p m t", t=PACK),
+            in_=wb_raw[:].bitcast(U16).rearrange("p (m t) -> p m t", t=PACK),
+        )
+        nc.vector.tensor_copy(
+            out=wb_plane[:].rearrange("p (t m) -> p m t", t=PACK),
+            in_=wbs_raw[:].bitcast(U8).rearrange("p (m t) -> p m t", t=PACK),
+        )
 
         a_sb = sb.tile([P, PACK, J], F32, name="a_sb")
         peak = sb.tile([P, PACK], F32, name="peak")

from contextlib import ExitStack

import concourse.mybir as mybir

K, T, J, R, N = 1024, 1024, 256, 512, 512
FLOPS = 2 * K * R * J + 2 * R * N * J

F32 = mybir.dt.float32
BF16 = mybir.dt.bfloat16
I32 = mybir.dt.int32
U32 = mybir.dt.uint32
U16 = mybir.dt.uint16
U8 = mybir.dt.uint8
E5M2X4 = mybir.dt.float8_e5m2_x4
E4M3X4 = mybir.dt.float8_e4m3fn_x4
E2M1X4 = mybir.dt.float4_e2m1fn_x4
ALU = mybir.AluOpType
ACT = mybir.ActivationFunctionType
AXIS = mybir.AxisListType

P = 128
PACK = 4
PASSES = K // (P * PACK)
QUADS = 4
LEAD = 8
HALF = J // 2
WALK = 4


def tile_list_steps_peakscaled_capped_pl_kernel(
    tc, xf, fk, w_words, w_scales, us, wb_words, wb_scales, hi, rw, offs, out_0, out_1, out_2
):
    nc = tc.nc
    with ExitStack() as ctx:
        sb = ctx.enter_context(tc.tile_pool(name="sb", bufs=1))
        shared = ctx.enter_context(tc.tile_pool(name="shared", bufs=1))
        ps = ctx.enter_context(tc.psum_pool(name="ps", bufs=1))

        offsets = sb.tile([P, J // 16], U16, name="offsets")
        w_raw = sb.tile([P, PASSES, R], I32, name="w_raw")
        ws_raw = sb.tile([P, PASSES, R // 4], I32, name="ws_raw")
        wb_raw = sb.tile([P, N // 2], I32, name="wb_raw")
        wbs_raw = sb.tile([P, N // 4], I32, name="wbs_raw")
        fk_sb = sb.tile([P, PASSES, PACK], F32, name="fk_sb")
        us_sb = sb.tile([P, PACK], F32, name="us_sb")
        hi_sb = sb.tile([P, PACK], F32, name="hi_sb")
        rw_sb = sb.tile([P, J], F32, name="rw_sb")
        picked = sb.tile([P, PASSES * PACK, LEAD + J], F32, name="picked")

        nc.vector.memset(ws_raw[:], 0)
        nc.vector.memset(wbs_raw[:], 0)
        zeros = sb.tile([P, PASSES * PACK, 1], F32, name="zeros")
        nc.vector.memset(zeros[:], 0.0)
        nc.scalar.activation(picked[:, :, LEAD - 1 : LEAD], zeros[:], ACT.Copy)

        x_rows = xf.rearrange("(g p t) c -> g p t c", g=PASSES, t=PACK)
        groups = [(g, t, 1) for g in range(PASSES) for t in range(PACK)]
        x_tiles = [sb.tile([P, n, T], F32, name="x_%d_%d" % (g, t0)) for g, t0, n in groups]

        def load_x(i):
            g, t0, n = groups[i]
            nc.sync.dma_start(out=x_tiles[i][:], in_=x_rows[g, :, t0 : t0 + n, :])

        nc.sync.dma_start(offsets[:], offs)
        nc.sync.dma_start(out=fk_sb[:], in_=fk.rearrange("(g p t) o -> p g (t o)", g=PASSES, t=PACK))
        nc.sync.dma_start(out=w_raw[:], in_=w_words.rearrange("g p n t -> p g (n t)").bitcast(I32))
        ws_dram = w_scales.rearrange("g q c -> q g c").bitcast(I32)
        for q in range(QUADS):
            nc.sync.dma_start(out=ws_raw[32 * q : 32 * q + 4, :, :], in_=ws_dram[4 * q : 4 * q + 4, :, :])
        for i in range(len(groups)):
            load_x(i)
        nc.sync.dma_start(out=wb_raw[:], in_=wb_words[0].bitcast(I32))
        wbs_dram = wb_scales[0].bitcast(I32)
        for q in range(QUADS):
            nc.sync.dma_start(out=wbs_raw[32 * q : 32 * q + 4, :], in_=wbs_dram[4 * q : 4 * q + 4, :])
        nc.sync.dma_start(out=us_sb[:], in_=us.rearrange("(p t) o -> p (t o)", t=PACK))
        nc.sync.dma_start(out=hi_sb[:], in_=hi.rearrange("(p t) o -> p (t o)", t=PACK))
        nc.sync.dma_start(out=rw_sb[:], in_=rw[0].partition_broadcast(P))

        w_codes = sb.tile([P, PASSES, R], U32, name="w_codes", align_bytes=64)
        w_plane = sb.tile([P, PASSES, R], U8, name="w_plane", align_bytes=64)
        nc.vector.tensor_copy(
            out=w_codes[:].rearrange("p g (t m) -> p g m t", t=PACK),
            in_=w_raw[:].bitcast(U32).rearrange("p g (m t) -> p g m t", t=PACK),
        )
        nc.vector.tensor_copy(
            out=w_plane[:].rearrange("p g (t m) -> p g m t", t=PACK),
            in_=ws_raw[:].bitcast(U8).rearrange("p g (m t) -> p g m t", t=PACK),
        )

        steps = sb.tile([P, PASSES * PACK, J], F32, name="steps")
        u_bf = [
            shared.tile([P, J, PACK], BF16, name="u_bf%d" % g, align_bytes=64, offset=g * J * PACK * 2)
            for g in range(PASSES)
        ]
        u_codes = [sb.tile([P, J], U32, name="u_codes%d" % g, align_bytes=64) for g in range(PASSES)]
        u_plane = [sb.tile([P, J], U8, name="u_plane%d" % g, align_bytes=64) for g in range(PASSES)]
        a_ps = [ps.tile([P, J], F32, name="a_ps%d" % t) for t in range(PACK)]

        def step_and_scale(g, t, spans):
            s = g * PACK + t
            for j0, j1 in spans:
                nc.vector.scalar_tensor_tensor(
                    out=steps[:, s, j0:j1],
                    in0=picked[:, s, LEAD - 1 + j0 : LEAD - 1 + j1],
                    scalar=-0.6,
                    in1=picked[:, s, LEAD + j0 : LEAD + j1],
                    op0=ALU.mult,
                    op1=ALU.add,
                )
            for j0, j1 in spans:
                nc.vector.tensor_scalar(
                    out=u_bf[g][:, j0:j1, t],
                    in0=steps[:, s, j0:j1],
                    scalar1=fk_sb[:, g, t : t + 1],
                    scalar2=None,
                    op0=ALU.mult,
                )

        def quantise(codes, plane, grouped, fmt, spans):
            for j0, j1 in spans:
                nc.vector.quantize_mx(
                    out=codes[:, j0:j1].bitcast(fmt),
                    scales=plane[:, j0:j1],
                    in_=grouped[:, j0:j1, :].rearrange("p j t -> p (j t)"),
                )

        whole = [(0, J)]
        halves = [(0, HALF), (HALF, J)]
        for i, (g, t0, n) in enumerate(groups):
            for d in range(n):
                t = t0 + d
                s = g * PACK + t
                window = x_tiles[i][:, d, :]
                if i < len(groups) - 1:
                    nc.scalar.activation(picked[:, s, LEAD:], window.indirect(offsets[:]), ACT.Copy)
                    step_and_scale(g, t, whole)
                else:
                    cols = HALF // 16
                    nc.vector.tensor_copy(picked[:, s, LEAD : LEAD + HALF], window.indirect(offsets[:, :cols]))
                    nc.scalar.activation(picked[:, s, LEAD + HALF :], window.indirect(offsets[:, cols:]), ACT.Copy)
                    step_and_scale(g, t, halves)
            if t0 + n == PACK:
                quantise(u_codes[g], u_plane[g], u_bf[g], E5M2X4, halves if g == PASSES - 1 else whole)
                for t in range(PACK):
                    cols = slice(t * P, (t + 1) * P)
                    nc.tensor.matmul_mx(
                        out=a_ps[t][:],
                        lhsT=w_codes[:, g, cols].bitcast(E5M2X4),
                        lhsT_scale=w_plane[:, g, cols],
                        rhs=u_codes[g][:].bitcast(E5M2X4),
                        rhs_scale=u_plane[g][:],
                        start=(g == 0),
                        stop=(g == PASSES - 1),
                    )

        last = (PASSES - 1) * J * PACK * 2
        wb_codes = shared.tile([P, N], U16, name="wb_codes", align_bytes=64, offset=last)
        wb_plane = shared.tile([P, N], U8, name="wb_plane", align_bytes=64, offset=last + 2 * N)
        nc.vector.tensor_copy(
            out=wb_codes[:].rearrange("p (t m) -> p m t", t=PACK),
            in_=wb_raw[:].bitcast(U16).rearrange("p (m t) -> p m t", t=PACK),
        )
        nc.vector.tensor_copy(
            out=wb_plane[:].rearrange("p (t m) -> p m t", t=PACK),
            in_=wbs_raw[:].bitcast(U8).rearrange("p (m t) -> p m t", t=PACK),
        )

        a_sb = sb.tile([P, PACK, J], F32, name="a_sb")
        peak = sb.tile([P, PACK], F32, name="peak")
        inv_peak = sb.tile([P, PACK], F32, name="inv_peak")
        gain = sb.tile([P, 2], F32, name="gain")
        hid_rows = sb.tile([P, PACK, J], BF16, name="hid_rows")
        hid_bf = sb.tile([P, J, PACK], BF16, name="hid_bf", align_bytes=64)
        for t in range(PACK):
            nc.scalar.activation(a_sb[:, t, :], a_ps[t][:], ACT.Copy)
            nc.vector.tensor_reduce(
                out=peak[:, t : t + 1], in_=a_sb[:, t, :], axis=AXIS.X, op=ALU.max, apply_absolute_value=True
            )
            if t == 1:
                nc.vector.reciprocal(out=inv_peak[:, 0:2], in_=peak[:, 0:2])
                nc.vector.tensor_tensor(out=gain[:], in0=inv_peak[:, 0:2], in1=us_sb[:, 0:2], op=ALU.mult)
            elif t > 1:
                nc.vector.reciprocal(out=inv_peak[:, t : t + 1], in_=peak[:, t : t + 1])
        for t in range(PACK):
            if t < 2:
                nc.scalar.activation(hid_rows[:, t, :], a_sb[:, t, :], ACT.Copy, scale=gain[:, t : t + 1])
            else:
                nc.vector.tensor_scalar(
                    out=hid_rows[:, t, :],
                    in0=a_sb[:, t, :],
                    scalar1=inv_peak[:, t : t + 1],
                    scalar2=us_sb[:, t : t + 1],
                    op0=ALU.mult,
                    op1=ALU.mult,
                )

        def weave(copy, grouped, rows, j0, j1):
            copy(
                out=grouped[:, j0:j1, :].rearrange("p (c i) t -> p c t i", i=WALK),
                in_=rows[:, :, j0:j1].rearrange("p t (c i) -> p c t i", i=WALK),
            )

        hid_codes = sb.tile([P, J], U32, name="hid_codes", align_bytes=64)
        hid_plane = sb.tile([P, J], U8, name="hid_plane", align_bytes=64)
        for j0, j1 in halves:
            weave(nc.vector.tensor_copy, hid_bf, hid_rows, j0, j1)
        quantise(hid_codes, hid_plane, hid_bf, E5M2X4, halves)

        neg_hi = sb.tile([P, PACK], F32, name="neg_hi")
        nc.scalar.activation(neg_hi[:], hi_sb[:], ACT.Copy, scale=-1.0)
        p_ps = [ps.tile([P, J], F32, name="p_ps%d" % t) for t in range(PACK)]
        excess = sb.tile([P, PACK, J], F32, name="excess")
        y = sb.tile([P, PACK, J], F32, name="y")
        out_rows = out_0.rearrange("(p t) j -> p t j", t=PACK)
        for t in range(PACK):
            nc.tensor.matmul_mx(
                out=p_ps[t][:],
                lhsT=wb_codes[:, t * P : (t + 1) * P].bitcast(E2M1X4),
                lhsT_scale=wb_plane[:, t * P : (t + 1) * P],
                rhs=hid_codes[:].bitcast(E5M2X4),
                rhs_scale=hid_plane[:],
                start=True,
                stop=True,
            )
            nc.scalar.activation(excess[:, t, :], p_ps[t][:], ACT.Identity, bias=neg_hi[:, t : t + 1])
            nc.vector.scalar_tensor_tensor(
                out=y[:, t, :], in0=excess[:, t, :], scalar=0.0, in1=rw_sb[:], op0=ALU.min, op1=ALU.mult
            )
            if t % 2 == 1:
                nc.sync.dma_start(out=out_rows[:, t - 1 : t + 1, :], in_=y[:, t - 1 : t + 1, :])

        y_bf = sb.tile([P, J, PACK], BF16, name="y_bf", align_bytes=64)
        y_codes = sb.tile([P, J], U32, name="y_codes", align_bytes=64)
        y_plane = sb.tile([P, J], U8, name="y_plane", align_bytes=64)
        split = 176
        weave(nc.vector.tensor_copy, y_bf, y, 0, split)
        weave(nc.scalar.copy, y_bf, y, split, J)
        quantise(y_codes, y_plane, y_bf, E4M3X4, halves)
        nc.sync.dma_start(out=out_1[0].rearrange("p c t -> p (c t)").bitcast(I32), in_=y_codes[:].bitcast(I32))
        plane_words = y_plane[:].bitcast(I32)
        scales_dram = out_2[0].bitcast(I32)
        for q in range(QUADS):
            queue = nc.scalar if q % 2 == 0 else nc.sync
            queue.dma_start(out=scales_dram[4 * q : 4 * q + 4, :], in_=plane_words[32 * q : 32 * q + 4, :])
